import numpy as np
import ml_dtypes


def mxq(x, axis, fmt="e4m3"):
    dtype, down = {"e4m3": (ml_dtypes.float8_e4m3fn, 7), "e5m2": (ml_dtypes.float8_e5m2, 14)}[fmt]
    v = np.moveaxis(np.asarray(x, np.float32).astype(ml_dtypes.bfloat16).astype(np.float64), axis, -1)
    blocks = v.reshape(v.shape[:-1] + (-1, 32))
    amax = np.abs(blocks).max(-1, keepdims=True)
    byte = np.maximum(np.where(amax > 0, np.frexp(amax)[1] - 1 + 127, 0) - down, 1)
    scale = np.exp2(byte - 127.0)
    codes = (blocks / scale).astype(np.float32).astype(dtype).astype(np.float64)
    return np.moveaxis((codes * scale).reshape(v.shape), -1, axis)


WIDE = False


def mx_kscale(k):
    if not WIDE:
        return np.ones(k)
    levels = np.array([10, -10, 5, -5, 0])
    if k % 512:
        return np.exp2(np.random.permutation(np.resize(levels, k // 32))).repeat(32)
    a = np.empty((k // 512, 16))
    for p in range(k // 512):
        a[p, :8] = np.random.permutation(np.resize(levels, 8))
        for g in range(8):
            far = levels[np.abs(levels - a[p, g]) >= 10]
            a[p, g + 8] = far[np.random.randint(len(far))]
    return np.exp2(a.ravel()).repeat(32)


def f64(x):
    return np.asarray(x).astype(np.float64)


def striped(idx):
    return np.tile(idx.reshape(-1, 16).T, (8, 1)).astype(np.uint16)


def unstriped(offs):
    return offs[:16].T.reshape(-1).astype(np.int64)


E2M1 = np.array([0.0, 0.5, 1.0, 1.5, 2.0, 3.0, 4.0, 6.0, -0.0, -0.5, -1.0, -1.5, -2.0, -3.0, -4.0, -6.0])


def pack_weight(w, fmt):
    k, n = w.shape
    w = f64(np.asarray(w, np.float32).astype(ml_dtypes.bfloat16)).reshape(k // 32, 32, n)
    amax = np.abs(w).max(1)
    if fmt == "e4m3":
        byte = np.frexp(amax)[1] - 1 + 127 - 7
    else:
        mant, ex = np.frexp(amax / 6.0)
        byte = np.where(mant > 0.5, ex, ex - 1) + 127
    byte = np.clip(np.where(amax > 0, byte, 1), 1, 254)
    scaled = (w * np.exp2(127.0 - byte)[:, None, :]).reshape(k, n).astype(np.float32)
    by_word = np.ascontiguousarray(scaled.reshape(k // 512, 128, 4, n).transpose(0, 1, 3, 2))
    if fmt == "e4m3":
        words = by_word.astype(ml_dtypes.float8_e4m3fn).view(np.uint8)
    else:
        c = by_word.astype(ml_dtypes.float4_e2m1fn).view(np.uint8) & 0xF
        words = (c[..., 0::2] | (c[..., 1::2] << 4)).reshape(k // 512, 128, 2 * n)
    return np.ascontiguousarray(words), np.ascontiguousarray(byte.astype(np.uint8).reshape(k // 512, 16, n))


def unpack_weight(words, scales, fmt):
    g, _, n = scales.shape
    words = np.ascontiguousarray(words).reshape(g, 128, n, -1)
    if fmt == "e4m3":
        vals = words.view(ml_dtypes.float8_e4m3fn).astype(np.float64)
    else:
        nib = np.empty((g, 128, n, 4), np.uint8)
        nib[..., 0::2] = words & 0xF
        nib[..., 1::2] = words >> 4
        vals = E2M1[nib]
    vals = vals * np.repeat(np.exp2(scales.astype(np.float64) - 127.0), 8, axis=1)[..., None]
    return vals.transpose(0, 1, 3, 2).reshape(g * 512, n)


def gelu(v):
    return 0.5 * v * (1.0 + np.tanh(np.sqrt(2.0 / np.pi) * (v + 0.044715 * v**3)))


def striped8(idx):
    return np.concatenate([v.reshape(-1, 16).T for v in idx]).astype(np.uint16)


def unstriped8(offs):
    return np.stack([offs[16 * g:16 * g + 16].T.reshape(-1) for g in range(8)]).astype(np.int64)


def put_heads(h, wgs, idx8, t2):
    r = np.arange(h.shape[0])
    page = np.zeros((h.shape[0], t2))
    page[r[:, None], idx8[r % 512 // 64]] = wgs[r // 4 % 128] * h
    return page


T, S, T2, K, H, N = 2048, 1024, 2048, 512, 1024, 512

def setup_inputs():
    n = np.random.standard_normal
    s = mx_kscale(K)[:, None]
    u = mx_kscale(H)[:, None]
    tab_words, tab_scales = pack_weight(n((K, T)) * s, "e4m3")
    w1 = n((K, H)) / np.sqrt(K) / s * np.sqrt(u.T)
    w4_words, w4_scales = pack_weight(n((K, H)) / np.sqrt(K) / s * np.sqrt(u.T), "e2m1")
    w8_words, w8_scales = pack_weight(0.4 * n((H, N)) / np.sqrt(H) / u, "e4m3")
    return {
        "tab_words": tab_words, "tab_scales": tab_scales,
        "offs": striped(np.random.permutation(T)[:S]),
        "offs2": striped8(np.stack([np.random.permutation(T2)[:S] for _ in range(8)])),
        "w1": w1.astype(np.float32),
        "w4_words": w4_words, "w4_scales": w4_scales,
        "wgs": np.repeat(np.random.uniform(0.5, 2.0, (8, S)), 16, axis=0).astype(np.float32),
        "recipe": (n((H, T2)) * u).astype(np.float32),
        "w8_words": w8_words, "w8_scales": w8_scales,
        "lim": np.random.uniform(0.5, 2.0, N).astype(np.float32),
    }

def reference(tab_words, tab_scales, offs, offs2, w1, w4_words, w4_scales, wgs, recipe, w8_words, w8_scales, lim):
    v = unpack_weight(tab_words, tab_scales, "e4m3")[:, unstriped(offs)]
    w4 = unpack_weight(w4_words, w4_scales, "e2m1")
    w8 = unpack_weight(w8_words, w8_scales, "e4m3")
    a = mxq(f64(w1), 0, "e4m3").T @ v
    b = w4.T @ v
    h = np.square(a) - np.square(b)
    page = put_heads(h, f64(wgs), unstriped8(offs2), T2)
    z = f64(recipe) - page
    y = w8.T @ mxq(z, 0, "e4m3")
    return f64(lim)[:, None] * np.tanh(y)

@@ -1,0 +1,293 @@
+from contextlib import ExitStack
+
+import concourse.mybir as mybir
+from concourse.masks import make_identity
+
+T, S, T2, K, H, N = 2048, 1024, 2048, 512, 1024, 512
+FLOPS = 2 * (2 * K * H * S + H * N * T2)
+
+F32 = mybir.dt.float32
+BF16 = mybir.dt.bfloat16
+I32 = mybir.dt.int32
+U32 = mybir.dt.uint32
+U16 = mybir.dt.uint16
+U8 = mybir.dt.uint8
+FP8X4 = mybir.dt.float8_e4m3fn_x4
+FP4X4 = mybir.dt.float4_e2m1fn_x4
+ACT = mybir.ActivationFunctionType
+ALU = mybir.AluOpType
+
+P = 128
+BANK = 512
+SLICES = 8
+
+
+def tile_list_wafer_overlay_correction_kernel(
+    tc, tab_words, tab_scales, offs, offs2, w1, w4_words, w4_scales, wgs, recipe, w8_words, w8_scales, lim, out
+):
+    nc = tc.nc
+    with ExitStack() as ctx:
+        lists = ctx.enter_context(tc.tile_pool(name="lists", bufs=1))
+        keep = ctx.enter_context(tc.tile_pool(name="keep", bufs=1))
+        ring = ctx.enter_context(tc.tile_pool(name="ring", bufs=2))
+        psum = ctx.enter_context(tc.psum_pool(name="psum", bufs=2))
+
+        def held(name, cols, dtype, tag=None):
+            return keep.tile([P, cols], dtype, name=name, tag=tag or name, align_bytes=64)
+
+        picks = lists.tile([P, S // 16], U16, name="picks")
+        places = lists.tile([P, S // 16], U16, name="places")
+
+        tab = held("tab", T, I32, "tab_then_page")
+        tab_sc = held("tab_sc", T, U8)
+        w4_raw = held("w4_raw", 2 * H, U8)
+        w4_sc_raw = held("w4_sc_raw", H, U8)
+        w8 = held("w8", 2 * N, I32)
+        w8_sc = held("w8_sc", 2 * N, U8)
+        wgt = held("wgt", S, F32)
+        lim_col = held("lim_col", N // P, F32)
+        ident = held("ident", P, F32)
+        w1_raw = [keep.tile([P, 4, 256], F32, name="w1_raw%d" % q, align_bytes=64) for q in range(4)]
+
+        for plane in (tab_sc, w4_sc_raw, w8_sc):
+            nc.vector.memset(plane[:].bitcast(I32), 0)
+        pages = [held("page0", T2, F32), held("page1", T2, F32)]
+        for page in pages:
+            nc.vector.memset(page[:], 0.0)
+        make_identity(nc, ident[:])
+        warm = held("warm", 1, F32)
+        nc.scalar.activation(out=warm[:], in_=ident[:, 0:1], func=ACT.Tanh)
+
+        def load_w1(q):
+            nc.sync.dma_start(out=w1_raw[q][:], in_=w1[:, 256 * q : 256 * (q + 1)].rearrange("(p j) c -> p j c", j=4))
+
+        load_w1(0)
+        load_w1(1)
+        nc.sync.dma_start(picks[:], offs)
+        for q in range(4):
+            nc.sync.dma_start(out=tab_sc[32 * q : 32 * q + 4, :].bitcast(I32), in_=tab_scales[0, 4 * q : 4 * q + 4, :].bitcast(I32))
+        nc.sync.dma_start(out=tab[:], in_=tab_words[0].rearrange("p t i -> p (t i)").bitcast(I32))
+        nc.sync.dma_start(out=w4_raw[:].bitcast(I32), in_=w4_words[0].bitcast(I32))
+        for q in range(4):
+            nc.sync.dma_start(out=w4_sc_raw[32 * q : 32 * q + 4, :].bitcast(I32), in_=w4_scales[0, 4 * q : 4 * q + 4, :].bitcast(I32))
+        nc.sync.dma_start(places[:], offs2)
+        nc.sync.dma_start(out=wgt[:], in_=wgs)
+        load_w1(2)
+        load_w1(3)
+
+        rec_rows = recipe.rearrange("(b p i) m -> b i p m", b=2, i=4)
+        rec = {}
+
+        def load_recipe(s):
+            rec[s] = ring.tile([P, T2], F32, name="rec", bufs=4, align_bytes=64)
+            nc.sync.dma_start(out=rec[s][:], in_=rec_rows[s // 4, s % 4])
+
+        load_recipe(0)
+        load_recipe(1)
+        nc.sync.dma_start(
+            out=w8[:].rearrange("p (a c) -> p a c", a=2),
+            in_=w8_words.rearrange("a p c i -> p a (c i)").bitcast(I32),
+        )
+        for q in range(4):
+            nc.sync.dma_start(
+                out=w8_sc[32 * q : 32 * q + 4, :].bitcast(I32).rearrange("p (a c) -> p a c", a=2),
+                in_=w8_scales[:, 4 * q : 4 * q + 4, :].rearrange("a r c -> r a c").bitcast(I32),
+            )
+        with nc.allow_non_contiguous_dma(reason="one limit for each partition"):
+            nc.sync.dma_start(out=lim_col[:], in_=lim.rearrange("(c p) -> p c", p=P))
+        load_recipe(2)
+        load_recipe(3)
+
+        v_codes = [held("v_codes%d" % hh, BANK, U32) for hh in range(2)]
+        v_sc = [held("v_sc%d" % hh, BANK, U8) for hh in range(2)]
+
+        def gather_words(hh):
+            nc.vector.tensor_copy(out=v_codes[hh][:], in_=tab[:].bitcast(U32).indirect(picks[:, 32 * hh : 32 * (hh + 1)]))
+
+        def gather_scales(hh):
+            nc.vector.tensor_copy(out=v_sc[hh][:], in_=tab_sc[:].indirect(picks[:, 32 * hh : 32 * (hh + 1)]))
+
+        w1_bf = [held("w1_bf0", 2048, BF16, "w1_then_page"), held("w1_bf1", 2048, BF16)]
+        w1_codes = [held("w1_codes%d" % b, 512, U32) for b in range(2)]
+        w1_sc = [held("w1_sc%d" % b, 512, U8) for b in range(2)]
+        w4 = [held("w4_%d" % b, 1024, U8) for b in range(2)]
+        w4_sc = [held("w4_sc%d" % b, 512, U8) for b in range(2)]
+
+        def round_w1(b):
+            for hq in range(2):
+                dst = w1_bf[b][:].rearrange("p (i m j) -> p m i j", i=4, j=4)[:, 64 * hq : 64 * (hq + 1)]
+                nc.scalar.copy(out=dst, in_=w1_raw[2 * b + hq][:].rearrange("p j (m i) -> p m i j", i=4))
+
+        def quantize_w1(b):
+            nc.vector.quantize_mx(out=w1_codes[b][:].bitcast(FP8X4), scales=w1_sc[b][:], in_=w1_bf[b][:])
+
+        def order_w4(b):
+            nc.vector.tensor_copy(
+                out=w4[b][:].bitcast(U16).rearrange("p (i m) -> p i m", i=4),
+                in_=w4_raw[:, 1024 * b : 1024 * (b + 1)].bitcast(U16).rearrange("p (m i) -> p i m", i=4),
+            )
+            nc.vector.tensor_copy(
+                out=w4_sc[b][:].rearrange("p (i m) -> p i m", i=4),
+                in_=w4_sc_raw[:, 512 * b : 512 * (b + 1)].rearrange("p (m i) -> p i m", i=4),
+            )
+
+        sq = {}
+
+        def squares(s):
+            b, i = divmod(s, 4)
+            cols = slice(P * i, P * (i + 1))
+            a2 = ring.tile([P, S], F32, name="a2")
+            b2 = ring.tile([P, S], F32, name="b2")
+            for hh in range(2):
+                half = slice(BANK * hh, BANK * (hh + 1))
+                acc_a = psum.tile([P, BANK], F32, name="acc_a", tag="mx", bufs=4)
+                nc.tensor.matmul_mx(
+                    out=acc_a[:], lhsT=w1_codes[b][:, cols].bitcast(FP8X4), lhsT_scale=w1_sc[b][:, cols],
+                    rhs=v_codes[hh][:].bitcast(FP8X4), rhs_scale=v_sc[hh][:], start=True, stop=True,
+                )
+                nc.scalar.activation(out=a2[:, half], in_=acc_a[:], func=ACT.Square)
+                acc_b = psum.tile([P, BANK], F32, name="acc_b", tag="mx", bufs=4)
+                nc.tensor.matmul_mx(
+                    out=acc_b[:], lhsT=w4[b][:, 2 * P * i : 2 * P * (i + 1)].bitcast(FP4X4), lhsT_scale=w4_sc[b][:, cols],
+                    rhs=v_codes[hh][:].bitcast(FP8X4), rhs_scale=v_sc[hh][:], start=True, stop=True,
+                )
+                nc.scalar.activation(out=b2[:, half], in_=acc_b[:], func=ACT.Square)
+            sq[s] = (a2, b2)
+
+        neg_h = {}
+
+        def difference(s, lo, hi, eng=nc.gpsimd):
+            a2, b2 = sq[s]
+            if s not in neg_h:
+                neg_h[s] = ring.tile([P, S], F32, name="neg_h", bufs=3)
+            eng.tensor_tensor(out=b2[:, lo:hi], in0=b2[:, lo:hi], in1=a2[:, lo:hi], op=ALU.subtract)
+            eng.tensor_tensor(out=neg_h[s][:, lo:hi], in0=b2[:, lo:hi], in1=wgt[:, lo:hi], op=ALU.mult)
+
+        def scatter(s, lo, hi):
+            window = pages[s % 4][:].indirect(places[:, lo // 16 : hi // 16])
+            nc.vector.tensor_copy(out=window, in_=neg_h[s][:, lo:hi])
+
+        z_turned = [[held("z_turned%d_%d" % (u, k), 512, BF16) for k in range(8)] for u in range(2)]
+        z_words = [[held("z_words%d_%d" % (b, c), 2048, BF16) for c in range(4)] for b in range(2)]
+        z_codes = [[held("z_codes%d_%d" % (b, c), BANK, U32) for c in range(4)] for b in range(2)]
+        z_sc = [[held("z_sc%d_%d" % (b, c), BANK, U8) for c in range(4)] for b in range(2)]
+
+        def turn(b, u, k, n_e):
+            acc = psum.tile([P, 2, 2, P], F32, name="turn_acc", tag="turn")
+            for mm in range(2):
+                cols = slice(P * (2 * k + mm), P * (2 * k + mm + 1))
+                for e in range(n_e):
+                    s = 4 * b + 2 * u + e
+                    nc.tensor.matmul(acc[:, mm, e, :], lhsT=rec[s][:, cols], rhs=ident[:], is_transpose=True, start=True, stop=False)
+                    nc.tensor.matmul(acc[:, mm, e, :], lhsT=pages[s % 4][:, cols], rhs=ident[:], is_transpose=True, start=False, stop=True)
+            dst = z_turned[u][k][:].rearrange("q (mm p e) -> q mm p e", mm=2, e=2)
+            nc.scalar.copy(out=dst[:, :, :, 0:n_e], in_=acc[:, :, 0:n_e, :].rearrange("q mm e p -> q mm p e"))
+
+        def turn_back(b, k):
+            acc = psum.tile([P, 2, 2, P], F32, name="back_acc", tag="back")
+            for u in range(2):
+                words = z_turned[u][k][:].bitcast(F32)
+                for mm in range(2):
+                    nc.tensor.transpose(acc[:, u, mm, :], words[:, P * mm : P * (mm + 1)], ident[:])
+            dst = z_words[b][k // 2][:].bitcast(F32)[:, BANK * (k % 2) : BANK * (k % 2 + 1)]
+            nc.scalar.copy(out=dst.rearrange("p (m u) -> p m u", u=2), in_=acc[:].rearrange("p u mm m -> p (mm m) u"))
+
+        def quantize_z(b, c):
+            nc.vector.quantize_mx(out=z_codes[b][c][:].bitcast(FP8X4), scales=z_sc[b][c][:], in_=z_words[b][c][:])
+
+        last = {}
+
+        def last_sum(c):
+            cols = slice(BANK * c, BANK * (c + 1))
+            last[c] = held("z_last%d" % c, BANK, BF16)
+            nc.vector.tensor_tensor(out=last[c][:], in0=rec[7][:, cols], in1=pages[3][:, cols], op=ALU.add)
+
+        def last_weave(c):
+            nc.vector.tensor_copy(out=z_words[1][c][:].rearrange("p (m t) -> p m t", t=4)[:, :, 3], in_=last[c][:])
+
+        squashed = {}
+
+        def commands(c):
+            for nt in range(4):
+                acc = psum.tile([P, BANK], F32, name="acc_y", tag="mx", bufs=4)
+                for b in range(2):
+                    cols = slice(N * b + P * nt, N * b + P * (nt + 1))
+                    nc.tensor.matmul_mx(
+                        out=acc[:], lhsT=w8[:, cols].bitcast(FP8X4), lhsT_scale=w8_sc[:, cols],
+                        rhs=z_codes[b][c][:].bitcast(FP8X4), rhs_scale=z_sc[b][c][:], start=(b == 0), stop=(b == 1),
+                    )
+                squashed[c, nt] = ring.tile([P, BANK], F32, name="squashed", bufs=4)
+                nc.scalar.activation(out=squashed[c, nt][:], in_=acc[:], func=ACT.Tanh)
+
+        def limit(c):
+            for nt in range(4):
+                res = ring.tile([P, BANK], F32, name="res", bufs=4)
+                nc.vector.tensor_scalar(
+                    out=res[:], in0=squashed[c, nt][:], scalar1=lim_col[:, nt : nt + 1], scalar2=None, op0=ALU.mult
+                )
+                nc.sync.dma_start(out=out[P * nt : P * (nt + 1), BANK * c : BANK * (c + 1)], in_=res[:])
+
+        round_w1(0)
+        gather_scales(0)
+        gather_scales(1)
+        quantize_w1(0)
+        gather_words(0)
+        order_w4(0)
+        gather_words(1)
+        pages.append(held("page2", T2, F32, "tab_then_page"))
+        pages.append(held("page3", T2, F32, "w1_then_page"))
+        for page in pages[2:]:
+            nc.gpsimd.memset(page[:], 0.0)
+        squares(0)
+        difference(0, 0, BANK, nc.vector)
+        squares(1)
+        difference(0, BANK, S)
+        scatter(0, 0, BANK)
+        round_w1(1)
+        squares(2)
+        difference(1, 0, S)
+        scatter(0, BANK, S)
+        squares(3)
+        order_w4(1)
+        quantize_w1(1)
+        for s in range(1, SLICES):
+            if s + 1 < SLICES:
+                difference(s + 1, 0, S)
+            scatter(s, 0, S)
+            if s + 3 < SLICES:
+                squares(s + 3)
+            if s in (1, 3, 5):
+                for k in range(8):
+                    turn(s // 4, s % 4 // 2, k, 2)
+                    if s == 3:
+                        turn_back(0, k)
+                for nxt in (s + 3, s + 4):
+                    if nxt < SLICES:
+                        load_recipe(nxt)
+            if s == 5:
+                for c in range(4):
+                    quantize_z(0, c)
+            if s == 6:
+                for k in range(8):
+                    turn(1, 1, k, 1)
+                    turn_back(1, k)
+        last_sum(0)
+        last_sum(1)
+        last_weave(0)
+        last_sum(2)
+        quantize_z(1, 0)
+        commands(0)
+        last_weave(1)
+        last_sum(3)
+        quantize_z(1, 1)
+        commands(1)
+        last_weave(2)
+        limit(0)
+        quantize_z(1, 2)
+        commands(2)
+        last_weave(3)
+        limit(1)
+        quantize_z(1, 3)
+        commands(3)
+        limit(2)
+        limit(3)

@@ -20,6 +20,7 @@ ALU = mybir.AluOpType
 P = 128
 BANK = 512
 SLICES = 8
+PE_CHUNKS = 2
 
 
 def tile_list_wafer_overlay_correction_kernel(
@@ -29,8 +30,13 @@ def tile_list_wafer_overlay_correction_kernel(
     with ExitStack() as ctx:
         lists = ctx.enter_context(tc.tile_pool(name="lists", bufs=1))
         keep = ctx.enter_context(tc.tile_pool(name="keep", bufs=1))
-        ring = ctx.enter_context(tc.tile_pool(name="ring", bufs=2))
-        psum = ctx.enter_context(tc.psum_pool(name="psum", bufs=2))
+        psum = ctx.enter_context(tc.psum_pool(name="psum", bufs=1))
+        banks = [psum.tile([P, BANK], F32, name="bank%d" % j) for j in range(8)]
+        taken = []
+
+        def next_bank():
+            taken.append(len(taken))
+            return banks[taken[-1] % 4]
 
         def held(name, cols, dtype, tag=None):
             return keep.tile([P, cols], dtype, name=name, tag=tag or name, align_bytes=64)
@@ -38,65 +44,46 @@ def tile_list_wafer_overlay_correction_kernel(
         picks = lists.tile([P, S // 16], U16, name="picks")
         places = lists.tile([P, S // 16], U16, name="places")
 
-        tab = held("tab", T, I32, "tab_then_page")
         tab_sc = held("tab_sc", T, U8)
         w4_raw = held("w4_raw", 2 * H, U8)
         w4_sc_raw = held("w4_sc_raw", H, U8)
-        w8 = held("w8", 2 * N, I32)
-        w8_sc = held("w8_sc", 2 * N, U8)
-        wgt = held("wgt", S, F32)
-        lim_col = held("lim_col", N // P, F32)
         ident = held("ident", P, F32)
-        w1_raw = [keep.tile([P, 4, 256], F32, name="w1_raw%d" % q, align_bytes=64) for q in range(4)]
+        w1_raw = [keep.tile([P, 4, 256], F32, name="w1_raw%d" % q, tag="w1_then_pairs%d" % q, align_bytes=64) for q in range(2)]
 
-        for plane in (tab_sc, w4_sc_raw, w8_sc):
-            nc.vector.memset(plane[:].bitcast(I32), 0)
+        nc.vector.memset(tab_sc[:].bitcast(I32), 0)
         pages = [held("page0", T2, F32), held("page1", T2, F32)]
         for page in pages:
             nc.vector.memset(page[:], 0.0)
+        nc.vector.memset(w4_sc_raw[:].bitcast(I32), 0)
         make_identity(nc, ident[:])
-        warm = held("warm", 1, F32)
-        nc.scalar.activation(out=warm[:], in_=ident[:, 0:1], func=ACT.Tanh)
+        warm = held("warm", 1, F32, "tab_then_page")
+        nc.scalar.activation(out=warm[:], in_=pages[0][:, 0:1], func=ACT.Tanh)
+        tab = held("tab", T, I32, "tab_then_page")
 
         def load_w1(q):
-            nc.sync.dma_start(out=w1_raw[q][:], in_=w1[:, 256 * q : 256 * (q + 1)].rearrange("(p j) c -> p j c", j=4))
+            nc.sync.dma_start(out=w1_raw[q % 2][:], in_=w1[:, 256 * q : 256 * (q + 1)].rearrange("(p j) c -> p j c", j=4))
 
+        nc.sync.dma_start(picks[:], offs)
+        nc.sync.dma_start(places[:], offs2)
         load_w1(0)
         load_w1(1)
-        nc.sync.dma_start(picks[:], offs)
+        nc.sync.dma_start(out=w4_raw[:].bitcast(I32), in_=w4_words[0].bitcast(I32))
         for q in range(4):
             nc.sync.dma_start(out=tab_sc[32 * q : 32 * q + 4, :].bitcast(I32), in_=tab_scales[0, 4 * q : 4 * q + 4, :].bitcast(I32))
         nc.sync.dma_start(out=tab[:], in_=tab_words[0].rearrange("p t i -> p (t i)").bitcast(I32))
-        nc.sync.dma_start(out=w4_raw[:].bitcast(I32), in_=w4_words[0].bitcast(I32))
         for q in range(4):
             nc.sync.dma_start(out=w4_sc_raw[32 * q : 32 * q + 4, :].bitcast(I32), in_=w4_scales[0, 4 * q : 4 * q + 4, :].bitcast(I32))
-        nc.sync.dma_start(places[:], offs2)
-        nc.sync.dma_start(out=wgt[:], in_=wgs)
-        load_w1(2)
-        load_w1(3)
 
         rec_rows = recipe.rearrange("(b p i) m -> b i p m", b=2, i=4)
         rec = {}
+        rec_ring = []
+        a2_ring = [held("a2_r%d" % j, S, F32) for j in range(3)]
+        b2_ring = [held("b2_r%d" % j, S, F32) for j in range(3)]
+        h_ring = [held("neg_h%d" % j, S, F32) for j in range(3)]
 
         def load_recipe(s):
-            rec[s] = ring.tile([P, T2], F32, name="rec", bufs=4, align_bytes=64)
+            rec[s] = rec_ring[s % 4]
             nc.sync.dma_start(out=rec[s][:], in_=rec_rows[s // 4, s % 4])
-
-        load_recipe(0)
-        load_recipe(1)
-        nc.sync.dma_start(
-            out=w8[:].rearrange("p (a c) -> p a c", a=2),
-            in_=w8_words.rearrange("a p c i -> p a (c i)").bitcast(I32),
-        )
-        for q in range(4):
-            nc.sync.dma_start(
-                out=w8_sc[32 * q : 32 * q + 4, :].bitcast(I32).rearrange("p (a c) -> p a c", a=2),
-                in_=w8_scales[:, 4 * q : 4 * q + 4, :].rearrange("a r c -> r a c").bitcast(I32),
-            )
-        with nc.allow_non_contiguous_dma(reason="one limit for each partition"):
-            nc.sync.dma_start(out=lim_col[:], in_=lim.rearrange("(c p) -> p c", p=P))
-        load_recipe(2)
-        load_recipe(3)
 
         v_codes = [held("v_codes%d" % hh, BANK, U32) for hh in range(2)]
         v_sc = [held("v_sc%d" % hh, BANK, U8) for hh in range(2)]
@@ -116,16 +103,18 @@ def tile_list_wafer_overlay_correction_kernel(
         def round_w1(b):
             for hq in range(2):
                 dst = w1_bf[b][:].rearrange("p (i m j) -> p m i j", i=4, j=4)[:, 64 * hq : 64 * (hq + 1)]
-                nc.scalar.copy(out=dst, in_=w1_raw[2 * b + hq][:].rearrange("p j (m i) -> p m i j", i=4))
+                nc.scalar.copy(out=dst, in_=w1_raw[hq][:].rearrange("p j (m i) -> p m i j", i=4))
 
         def quantize_w1(b):
             nc.vector.quantize_mx(out=w1_codes[b][:].bitcast(FP8X4), scales=w1_sc[b][:], in_=w1_bf[b][:])
 
-        def order_w4(b):
+        def order_w4_words(b):
             nc.vector.tensor_copy(
                 out=w4[b][:].bitcast(U16).rearrange("p (i m) -> p i m", i=4),
                 in_=w4_raw[:, 1024 * b : 1024 * (b + 1)].bitcast(U16).rearrange("p (m i) -> p i m", i=4),
             )
+
+        def order_w4_scales(b):
             nc.vector.tensor_copy(
                 out=w4_sc[b][:].rearrange("p (i m) -> p i m", i=4),
                 in_=w4_sc_raw[:, 512 * b : 512 * (b + 1)].rearrange("p (m i) -> p i m", i=4),
@@ -136,17 +125,16 @@ def tile_list_wafer_overlay_correction_kernel(
         def squares(s):
             b, i = divmod(s, 4)
             cols = slice(P * i, P * (i + 1))
-            a2 = ring.tile([P, S], F32, name="a2")
-            b2 = ring.tile([P, S], F32, name="b2")
+            a2, b2 = a2_ring[s % 3], b2_ring[s % 3]
             for hh in range(2):
                 half = slice(BANK * hh, BANK * (hh + 1))
-                acc_a = psum.tile([P, BANK], F32, name="acc_a", tag="mx", bufs=4)
+                acc_a = next_bank()
                 nc.tensor.matmul_mx(
                     out=acc_a[:], lhsT=w1_codes[b][:, cols].bitcast(FP8X4), lhsT_scale=w1_sc[b][:, cols],
                     rhs=v_codes[hh][:].bitcast(FP8X4), rhs_scale=v_sc[hh][:], start=True, stop=True,
                 )
                 nc.scalar.activation(out=a2[:, half], in_=acc_a[:], func=ACT.Square)
-                acc_b = psum.tile([P, BANK], F32, name="acc_b", tag="mx", bufs=4)
+                acc_b = next_bank()
                 nc.tensor.matmul_mx(
                     out=acc_b[:], lhsT=w4[b][:, 2 * P * i : 2 * P * (i + 1)].bitcast(FP4X4), lhsT_scale=w4_sc[b][:, cols],
                     rhs=v_codes[hh][:].bitcast(FP8X4), rhs_scale=v_sc[hh][:], start=True, stop=True,
@@ -155,85 +143,124 @@ def tile_list_wafer_overlay_correction_kernel(
             sq[s] = (a2, b2)
 
         neg_h = {}
+        gap = held("gap", S, F32)
 
         def difference(s, lo, hi, eng=nc.gpsimd):
             a2, b2 = sq[s]
-            if s not in neg_h:
-                neg_h[s] = ring.tile([P, S], F32, name="neg_h", bufs=3)
-            eng.tensor_tensor(out=b2[:, lo:hi], in0=b2[:, lo:hi], in1=a2[:, lo:hi], op=ALU.subtract)
-            eng.tensor_tensor(out=neg_h[s][:, lo:hi], in0=b2[:, lo:hi], in1=wgt[:, lo:hi], op=ALU.mult)
+            neg_h[s] = h_ring[s % 3]
+            eng.tensor_tensor(out=gap[:, lo:hi], in0=b2[:, lo:hi], in1=a2[:, lo:hi], op=ALU.subtract)
+            eng.tensor_tensor(out=neg_h[s][:, lo:hi], in0=gap[:, lo:hi], in1=wgt[:, lo:hi], op=ALU.mult)
 
         def scatter(s, lo, hi):
             window = pages[s % 4][:].indirect(places[:, lo // 16 : hi // 16])
             nc.vector.tensor_copy(out=window, in_=neg_h[s][:, lo:hi])
 
         z_turned = [[held("z_turned%d_%d" % (u, k), 512, BF16) for k in range(8)] for u in range(2)]
-        z_words = [[held("z_words%d_%d" % (b, c), 2048, BF16) for c in range(4)] for b in range(2)]
-        z_codes = [[held("z_codes%d_%d" % (b, c), BANK, U32) for c in range(4)] for b in range(2)]
+        z_words = {(0, c): held("z_words0_%d" % c, 2048, BF16) for c in range(4)}
+        z_codes = {(1, c): held("z_codes1_%d" % c, BANK, U32)[:] for c in range(4)}
         z_sc = [[held("z_sc%d_%d" % (b, c), BANK, U8) for c in range(4)] for b in range(2)]
+        pairs = {}
 
-        def turn(b, u, k, n_e):
-            acc = psum.tile([P, 2, 2, P], F32, name="turn_acc", tag="turn")
+        def turn(b, u, k):
+            acc = next_bank()[:].rearrange("q (mm e p) -> q mm e p", mm=2, e=2)
             for mm in range(2):
                 cols = slice(P * (2 * k + mm), P * (2 * k + mm + 1))
-                for e in range(n_e):
+                for e in range(2):
                     s = 4 * b + 2 * u + e
-                    nc.tensor.matmul(acc[:, mm, e, :], lhsT=rec[s][:, cols], rhs=ident[:], is_transpose=True, start=True, stop=False)
-                    nc.tensor.matmul(acc[:, mm, e, :], lhsT=pages[s % 4][:, cols], rhs=ident[:], is_transpose=True, start=False, stop=True)
+                    nc.tensor.matmul(acc[:, mm, e, :], lhsT=pages[s % 4][:, cols], rhs=ident[:], is_transpose=True, start=True, stop=False)
+                    nc.tensor.matmul(acc[:, mm, e, :], lhsT=rec[s][:, cols], rhs=ident[:], is_transpose=True, start=False, stop=True)
             dst = z_turned[u][k][:].rearrange("q (mm p e) -> q mm p e", mm=2, e=2)
-            nc.scalar.copy(out=dst[:, :, :, 0:n_e], in_=acc[:, :, 0:n_e, :].rearrange("q mm e p -> q mm p e"))
+            nc.scalar.copy(out=dst, in_=acc.rearrange("q mm e p -> q mm p e"))
 
-        def turn_back(b, k):
-            acc = psum.tile([P, 2, 2, P], F32, name="back_acc", tag="back")
+        def turn_back(k):
+            acc = next_bank()[:].rearrange("p (u mm m) -> p u mm m", u=2, mm=2)
             for u in range(2):
                 words = z_turned[u][k][:].bitcast(F32)
                 for mm in range(2):
                     nc.tensor.transpose(acc[:, u, mm, :], words[:, P * mm : P * (mm + 1)], ident[:])
-            dst = z_words[b][k // 2][:].bitcast(F32)[:, BANK * (k % 2) : BANK * (k % 2 + 1)]
-            nc.scalar.copy(out=dst.rearrange("p (m u) -> p m u", u=2), in_=acc[:].rearrange("p u mm m -> p (mm m) u"))
+            dst = z_words[0, k // 2][:].bitcast(F32)[:, BANK * (k % 2) : BANK * (k % 2 + 1)]
+            nc.scalar.copy(out=dst.rearrange("p (m u) -> p m u", u=2), in_=acc.rearrange("p u mm m -> p (mm m) u"))
+
+        def turn_back_pair(c):
+            acc = next_bank()
+            for mb in range(4):
+                words = z_turned[0][2 * c + mb // 2][:].bitcast(F32)
+                nc.tensor.transpose(acc[:, P * mb : P * (mb + 1)], words[:, P * (mb % 2) : P * (mb % 2 + 1)], ident[:])
+            nc.scalar.copy(out=pairs[c][:].bitcast(F32)[:, 0:BANK], in_=acc[:])
 
         def quantize_z(b, c):
-            nc.vector.quantize_mx(out=z_codes[b][c][:].bitcast(FP8X4), scales=z_sc[b][c][:], in_=z_words[b][c][:])
+            nc.vector.quantize_mx(out=z_codes[b, c].bitcast(FP8X4), scales=z_sc[b][c][:], in_=z_words[b, c][:])
 
-        last = {}
+        def chunk(c):
+            return slice(BANK * c, BANK * (c + 1))
+
+        planes = {}
+
+        def pair_tag(c):
+            return ("w1_then_pairs%d" if c < PE_CHUNKS else "z_turned0_%d") % c
+
+        def plane_sum(s, c):
+            at = c if s == 6 else 2 * (c - PE_CHUNKS) + s % 2
+            nc.gpsimd.tensor_tensor(
+                out=planes[s // 2][:, chunk(at)], in0=rec[s][:, chunk(c)], in1=pages[s % 4][:, chunk(c)], op=ALU.add
+            )
+
+        def pair_slots(u, c):
+            return pairs[c][:, 2 * BANK * u : 2 * BANK * (u + 1)].rearrange("p (m e) -> p m e", e=2)
 
         def last_sum(c):
-            cols = slice(BANK * c, BANK * (c + 1))
-            last[c] = held("z_last%d" % c, BANK, BF16)
-            nc.vector.tensor_tensor(out=last[c][:], in0=rec[7][:, cols], in1=pages[3][:, cols], op=ALU.add)
+            nc.vector.tensor_tensor(out=pair_slots(1, c)[:, :, 1], in0=rec[7][:, chunk(c)], in1=pages[3][:, chunk(c)], op=ALU.add)
 
         def last_weave(c):
-            nc.vector.tensor_copy(out=z_words[1][c][:].rearrange("p (m t) -> p m t", t=4)[:, :, 3], in_=last[c][:])
+            z_words[1, c] = held("z_words1_%d" % c, 2048, BF16)
+            nc.vector.tensor_copy(
+                out=z_words[1, c][:].bitcast(F32).rearrange("p (m u) -> p m u", u=2),
+                in_=pairs[c][:].bitcast(F32).rearrange("p (u m) -> p m u", u=2),
+            )
 
         squashed = {}
 
         def commands(c):
+            result = held("result%d" % c, T2, F32, ("w4_sc_raw", "tab_sc", "page0", "page1")[c])
             for nt in range(4):
-                acc = psum.tile([P, BANK], F32, name="acc_y", tag="mx", bufs=4)
+                acc = banks[(4 + 4 * c + nt) % 8]
                 for b in range(2):
                     cols = slice(N * b + P * nt, N * b + P * (nt + 1))
                     nc.tensor.matmul_mx(
                         out=acc[:], lhsT=w8[:, cols].bitcast(FP8X4), lhsT_scale=w8_sc[:, cols],
-                        rhs=z_codes[b][c][:].bitcast(FP8X4), rhs_scale=z_sc[b][c][:], start=(b == 0), stop=(b == 1),
+                        rhs=z_codes[b, c].bitcast(FP8X4), rhs_scale=z_sc[b][c][:], start=(b == 0), stop=(b == 1),
                     )
-                squashed[c, nt] = ring.tile([P, BANK], F32, name="squashed", bufs=4)
-                nc.scalar.activation(out=squashed[c, nt][:], in_=acc[:], func=ACT.Tanh)
+                squashed[c, nt] = result[:, chunk(nt)]
+                nc.scalar.activation(out=squashed[c, nt], in_=acc[:], func=ACT.Tanh)
 
-        def limit(c):
-            for nt in range(4):
-                res = ring.tile([P, BANK], F32, name="res", bufs=4)
+        def limit(c, nt, on_scalar):
+            res = squashed[c, nt]
+            if on_scalar:
+                nc.scalar.activation(out=res, in_=res, func=ACT.Copy, scale=lim_col[:, nt : nt + 1])
+            else:
                 nc.vector.tensor_scalar(
-                    out=res[:], in0=squashed[c, nt][:], scalar1=lim_col[:, nt : nt + 1], scalar2=None, op0=ALU.mult
+                    out=res, in0=res, scalar1=lim_col[:, nt : nt + 1], scalar2=None, op0=ALU.mult
                 )
-                nc.sync.dma_start(out=out[P * nt : P * (nt + 1), BANK * c : BANK * (c + 1)], in_=res[:])
+            nc.sync.dma_start(out=out[P * nt : P * (nt + 1), chunk(c)], in_=res)
 
         round_w1(0)
+        order_w4_words(0)
+        order_w4_words(1)
+        wgt = held("wgt", S, F32, "w4_raw")
+        nc.sync.dma_start(out=wgt[:], in_=wgs)
         gather_scales(0)
         gather_scales(1)
         quantize_w1(0)
         gather_words(0)
-        order_w4(0)
+        order_w4_scales(0)
+        order_w4_scales(1)
         gather_words(1)
+        load_w1(2)
+        load_w1(3)
+        rec_ring.append(held("rec0", T2, F32, "w4_sc_raw"))
+        rec_ring.append(held("rec1", T2, F32, "tab_sc"))
+        load_recipe(0)
+        load_recipe(1)
         pages.append(held("page2", T2, F32, "tab_then_page"))
         pages.append(held("page3", T2, F32, "w1_then_page"))
         for page in pages[2:]:
@@ -244,50 +271,81 @@ def tile_list_wafer_overlay_correction_kernel(
         difference(0, BANK, S)
         scatter(0, 0, BANK)
         round_w1(1)
+        for c in range(PE_CHUNKS):
+            pairs[c] = held("pairs%d" % c, 2048, BF16, "w1_then_pairs%d" % c)
         squares(2)
-        difference(1, 0, S)
-        scatter(0, BANK, S)
         squares(3)
-        order_w4(1)
+        difference(1, 0, S)
+        difference(2, 0, S)
+        scatter(0, BANK, S)
         quantize_w1(1)
+        rec_ring.append(held("rec2", T2, F32, "w1_bf1"))
+        rec_ring.append(held("rec3", T2, F32, "w4_0"))
+        load_recipe(2)
+        load_recipe(3)
+        w8 = held("w8", 2 * N, I32, "w1_codes0")
+        w8_sc = held("w8_sc", 2 * N, U8, "w1_sc0")
+        lim_col = held("lim_col", N // P, F32, "w4_sc0")
+        nc.gpsimd.memset(w8_sc[:].bitcast(I32), 0)
+        nc.sync.dma_start(
+            out=w8[:].rearrange("p (a c) -> p a c", a=2),
+            in_=w8_words.rearrange("a p c i -> p a (c i)").bitcast(I32),
+        )
+        for q in range(4):
+            nc.sync.dma_start(
+                out=w8_sc[32 * q : 32 * q + 4, :].bitcast(I32).rearrange("p (a c) -> p a c", a=2),
+                in_=w8_scales[:, 4 * q : 4 * q + 4, :].rearrange("a r c -> r a c").bitcast(I32),
+            )
+        with nc.allow_non_contiguous_dma(reason="one limit for each partition"):
+            nc.sync.dma_start(out=lim_col[:], in_=lim.rearrange("(c p) -> p c", p=P))
+        squares(4)
+        squares(5)
         for s in range(1, SLICES):
-            if s + 1 < SLICES:
-                difference(s + 1, 0, S)
+            if s + 2 < SLICES:
+                difference(s + 2, 0, S)
             scatter(s, 0, S)
-            if s + 3 < SLICES:
-                squares(s + 3)
-            if s in (1, 3, 5):
+            if s in (1, 3):
                 for k in range(8):
-                    turn(s // 4, s % 4 // 2, k, 2)
-                    if s == 3:
-                        turn_back(0, k)
-                for nxt in (s + 3, s + 4):
-                    if nxt < SLICES:
-                        load_recipe(nxt)
+                    turn(0, s // 2, k)
+                load_recipe(s + 3)
+                load_recipe(s + 4)
+            if s == 2:
+                squares(6)
+                squares(7)
+            if s == 3:
+                for k in range(8):
+                    turn_back(k)
             if s == 5:
-                for c in range(4):
-                    quantize_z(0, c)
+                for k in range(2 * PE_CHUNKS):
+                    turn(1, 0, k)
+                for c in range(PE_CHUNKS):
+                    turn_back_pair(c)
             if s == 6:
-                for k in range(8):
-                    turn(1, 1, k, 1)
-                    turn_back(1, k)
+                planes[2] = held("planes45", T2, BF16, "gap")
+                planes[3] = held("plane6", T2, BF16, "z_turned0_1")
+                for c in range(PE_CHUNKS, 4):
+                    pairs[c] = held("pairs%d" % c, 2048, BF16, "z_turned0_%d" % c)
+                for c in range(PE_CHUNKS, 4):
+                    plane_sum(4, c)
+                for c in range(PE_CHUNKS, 4):
+                    plane_sum(5, c)
+                    nc.scalar.copy(out=pair_slots(0, c), in_=planes[2][:, 2 * BANK * (c - PE_CHUNKS) : 2 * BANK * (c - PE_CHUNKS + 1)].rearrange("p (e m) -> p m e", e=2))
+                for c in range(4):
+                    plane_sum(6, c)
+                    nc.scalar.copy(out=pair_slots(1, c), in_=planes[3][:, chunk(c)].unsqueeze(2).to_broadcast([P, BANK, 2]))
         last_sum(0)
-        last_sum(1)
-        last_weave(0)
-        last_sum(2)
-        quantize_z(1, 0)
-        commands(0)
-        last_weave(1)
-        last_sum(3)
-        quantize_z(1, 1)
-        commands(1)
-        last_weave(2)
-        limit(0)
-        quantize_z(1, 2)
-        commands(2)
-        last_weave(3)
-        limit(1)
-        quantize_z(1, 3)
-        commands(3)
-        limit(2)
-        limit(3)
+        for c in range(4):
+            last_weave(c)
+            z_codes[0, c] = held("z_codes0_%d" % c, BANK, U32, pair_tag(c))[:]
+            quantize_z(0, c)
+            quantize_z(1, c)
+            if c + 1 < 4:
+                last_sum(c + 1)
+            commands(c)
+            if c >= 1:
+                for nt in range(3):
+                    limit(c - 1, nt, False)
+            if c + 1 < 4:
+                limit(c, 3, True)
+        for nt in range(4):
+            limit(3, nt, False)

@@ -19,8 +19,16 @@ ALU = mybir.AluOpType
 
 P = 128
 BANK = 512
-SLICES = 8
-PE_CHUNKS = 2
+PACK = 4
+SLICES = H // P
+CHUNKS = T2 // BANK
+STRIPS = T2 // (2 * P)
+W1_COLS = 256
+PAGES = 4
+AHEAD = 3
+TURNED_CHUNKS = 1
+SCALAR_LIMITS = [(c, nt) for c in range(2) for nt in (2, 3)]
+FIRST_CHUNKS = 2
 
 
 def tile_list_wafer_overlay_correction_kernel(
@@ -38,17 +46,23 @@ def tile_list_wafer_overlay_correction_kernel(
             taken.append(len(taken))
             return banks[taken[-1] % 4]
 
-        def held(name, cols, dtype, tag=None):
-            return keep.tile([P, cols], dtype, name=name, tag=tag or name, align_bytes=64)
+        def held(name, cols, dtype, after=None):
+            return keep.tile([P, cols], dtype, name=name, tag=after or name, align_bytes=64)
+
+        def chunk(c):
+            return slice(BANK * c, BANK * (c + 1))
+
+        def scale_rows(plane, q):
+            return plane[32 * q : 32 * q + 4, :].bitcast(I32)
 
         picks = lists.tile([P, S // 16], U16, name="picks")
         places = lists.tile([P, S // 16], U16, name="places")
-
+        tab = held("tab", T, I32)
         tab_sc = held("tab_sc", T, U8)
         w4_raw = held("w4_raw", 2 * H, U8)
         w4_sc_raw = held("w4_sc_raw", H, U8)
         ident = held("ident", P, F32)
-        w1_raw = [keep.tile([P, 4, 256], F32, name="w1_raw%d" % q, tag="w1_then_pairs%d" % q, align_bytes=64) for q in range(2)]
+        w1_raw = [keep.tile([P, PACK, W1_COLS], F32, name="w1_raw%d" % j, align_bytes=64) for j in range(2)]
 
         nc.vector.memset(tab_sc[:].bitcast(I32), 0)
         pages = [held("page0", T2, F32), held("page1", T2, F32)]
@@ -56,236 +70,250 @@ def tile_list_wafer_overlay_correction_kernel(
             nc.vector.memset(page[:], 0.0)
         nc.vector.memset(w4_sc_raw[:].bitcast(I32), 0)
         make_identity(nc, ident[:])
-        warm = held("warm", 1, F32, "tab_then_page")
-        nc.scalar.activation(out=warm[:], in_=pages[0][:, 0:1], func=ACT.Tanh)
-        tab = held("tab", T, I32, "tab_then_page")
 
-        def load_w1(q):
-            nc.sync.dma_start(out=w1_raw[q % 2][:], in_=w1[:, 256 * q : 256 * (q + 1)].rearrange("(p j) c -> p j c", j=4))
+        def load_w1(b):
+            for j in range(2):
+                cols = slice(BANK * b + W1_COLS * j, BANK * b + W1_COLS * (j + 1))
+                nc.sync.dma_start(out=w1_raw[j][:], in_=w1[:, cols].rearrange("(p t) c -> p t c", t=PACK))
 
         nc.sync.dma_start(picks[:], offs)
+        nc.sync.dma_start(out=w4_raw[:].bitcast(I32), in_=w4_words[0].bitcast(I32))
+        nc.sync.dma_start(out=tab[:], in_=tab_words[0].rearrange("p t i -> p (t i)").bitcast(I32))
         nc.sync.dma_start(places[:], offs2)
         load_w1(0)
-        load_w1(1)
-        nc.sync.dma_start(out=w4_raw[:].bitcast(I32), in_=w4_words[0].bitcast(I32))
         for q in range(4):
-            nc.sync.dma_start(out=tab_sc[32 * q : 32 * q + 4, :].bitcast(I32), in_=tab_scales[0, 4 * q : 4 * q + 4, :].bitcast(I32))
-        nc.sync.dma_start(out=tab[:], in_=tab_words[0].rearrange("p t i -> p (t i)").bitcast(I32))
+            nc.scalar.dma_start(out=scale_rows(tab_sc, q), in_=tab_scales[0, 4 * q : 4 * q + 4, :].bitcast(I32))
         for q in range(4):
-            nc.sync.dma_start(out=w4_sc_raw[32 * q : 32 * q + 4, :].bitcast(I32), in_=w4_scales[0, 4 * q : 4 * q + 4, :].bitcast(I32))
+            nc.sync.dma_start(out=scale_rows(w4_sc_raw, q), in_=w4_scales[0, 4 * q : 4 * q + 4, :].bitcast(I32))
 
-        rec_rows = recipe.rearrange("(b p i) m -> b i p m", b=2, i=4)
-        rec = {}
-        rec_ring = []
-        a2_ring = [held("a2_r%d" % j, S, F32) for j in range(3)]
-        b2_ring = [held("b2_r%d" % j, S, F32) for j in range(3)]
-        h_ring = [held("neg_h%d" % j, S, F32) for j in range(3)]
+        recipe_slices = recipe.rearrange("(b p i) m -> b i p m", b=2, i=PACK)
+        rec = []
 
         def load_recipe(s):
-            rec[s] = rec_ring[s % 4]
-            nc.sync.dma_start(out=rec[s][:], in_=rec_rows[s // 4, s % 4])
+            nc.sync.dma_start(out=rec[s % PAGES][:], in_=recipe_slices[s // PACK, s % PACK])
 
-        v_codes = [held("v_codes%d" % hh, BANK, U32) for hh in range(2)]
-        v_sc = [held("v_sc%d" % hh, BANK, U8) for hh in range(2)]
+        v_codes = [held("v_codes%d" % half, BANK, U32) for half in range(2)]
+        v_sc = [held("v_sc%d" % half, BANK, U8) for half in range(2)]
 
-        def gather_words(hh):
-            nc.vector.tensor_copy(out=v_codes[hh][:], in_=tab[:].bitcast(U32).indirect(picks[:, 32 * hh : 32 * (hh + 1)]))
+        def entries(half):
+            return picks[:, BANK // 16 * half : BANK // 16 * (half + 1)]
 
-        def gather_scales(hh):
-            nc.vector.tensor_copy(out=v_sc[hh][:], in_=tab_sc[:].indirect(picks[:, 32 * hh : 32 * (hh + 1)]))
+        def gather_words(half):
+            nc.vector.tensor_copy(out=v_codes[half][:], in_=tab[:].bitcast(U32).indirect(entries(half)))
 
-        w1_bf = [held("w1_bf0", 2048, BF16, "w1_then_page"), held("w1_bf1", 2048, BF16)]
-        w1_codes = [held("w1_codes%d" % b, 512, U32) for b in range(2)]
-        w1_sc = [held("w1_sc%d" % b, 512, U8) for b in range(2)]
-        w4 = [held("w4_%d" % b, 1024, U8) for b in range(2)]
-        w4_sc = [held("w4_sc%d" % b, 512, U8) for b in range(2)]
+        def gather_scales(half):
+            nc.vector.tensor_copy(out=v_sc[half][:], in_=tab_sc[:].indirect(entries(half)))
+
+        w1_bf = [held("w1_bf0", PACK * BANK, BF16)]
+        w1_codes = [held("w1_codes%d" % b, BANK, U32) for b in range(2)]
+        w1_sc = [held("w1_sc%d" % b, BANK, U8) for b in range(2)]
+        w4 = [held("w4_%d" % b, 2 * BANK, U8) for b in range(2)]
+        w4_sc = [held("w4_sc%d" % b, BANK, U8) for b in range(2)]
 
         def round_w1(b):
-            for hq in range(2):
-                dst = w1_bf[b][:].rearrange("p (i m j) -> p m i j", i=4, j=4)[:, 64 * hq : 64 * (hq + 1)]
-                nc.scalar.copy(out=dst, in_=w1_raw[hq][:].rearrange("p j (m i) -> p m i j", i=4))
+            grouped = w1_bf[b][:].rearrange("p (i c t) -> p c i t", i=PACK, t=PACK)
+            width = W1_COLS // PACK
+            for j in range(2):
+                nc.scalar.copy(
+                    out=grouped[:, width * j : width * (j + 1)],
+                    in_=w1_raw[j][:].rearrange("p t (c i) -> p c i t", i=PACK),
+                )
 
         def quantize_w1(b):
             nc.vector.quantize_mx(out=w1_codes[b][:].bitcast(FP8X4), scales=w1_sc[b][:], in_=w1_bf[b][:])
 
         def order_w4_words(b):
             nc.vector.tensor_copy(
-                out=w4[b][:].bitcast(U16).rearrange("p (i m) -> p i m", i=4),
-                in_=w4_raw[:, 1024 * b : 1024 * (b + 1)].bitcast(U16).rearrange("p (m i) -> p i m", i=4),
+                out=w4[b][:].bitcast(U16).rearrange("p (i c) -> p i c", i=PACK),
+                in_=w4_raw[:].bitcast(U16)[:, chunk(b)].rearrange("p (c i) -> p i c", i=PACK),
             )
 
         def order_w4_scales(b):
             nc.vector.tensor_copy(
-                out=w4_sc[b][:].rearrange("p (i m) -> p i m", i=4),
-                in_=w4_sc_raw[:, 512 * b : 512 * (b + 1)].rearrange("p (m i) -> p i m", i=4),
+                out=w4_sc[b][:].rearrange("p (i c) -> p i c", i=PACK),
+                in_=w4_sc_raw[:, chunk(b)].rearrange("p (c i) -> p i c", i=PACK),
             )
 
-        sq = {}
+        a2_ring = [held("a2_%d" % j, S, F32) for j in range(AHEAD)]
+        b2_ring = [held("b2_%d" % j, S, F32) for j in range(AHEAD)]
+        weighted = [held("weighted%d" % j, S, F32) for j in range(AHEAD)]
+        neg_h = held("neg_h", S, F32)
 
         def squares(s):
-            b, i = divmod(s, 4)
+            b, i = divmod(s, PACK)
             cols = slice(P * i, P * (i + 1))
-            a2, b2 = a2_ring[s % 3], b2_ring[s % 3]
-            for hh in range(2):
-                half = slice(BANK * hh, BANK * (hh + 1))
-                acc_a = next_bank()
-                nc.tensor.matmul_mx(
-                    out=acc_a[:], lhsT=w1_codes[b][:, cols].bitcast(FP8X4), lhsT_scale=w1_sc[b][:, cols],
-                    rhs=v_codes[hh][:].bitcast(FP8X4), rhs_scale=v_sc[hh][:], start=True, stop=True,
-                )
-                nc.scalar.activation(out=a2[:, half], in_=acc_a[:], func=ACT.Square)
-                acc_b = next_bank()
-                nc.tensor.matmul_mx(
-                    out=acc_b[:], lhsT=w4[b][:, 2 * P * i : 2 * P * (i + 1)].bitcast(FP4X4), lhsT_scale=w4_sc[b][:, cols],
-                    rhs=v_codes[hh][:].bitcast(FP8X4), rhs_scale=v_sc[hh][:], start=True, stop=True,
-                )
-                nc.scalar.activation(out=b2[:, half], in_=acc_b[:], func=ACT.Square)
-            sq[s] = (a2, b2)
+            for half in range(2):
+                for codes, scales, squared in (
+                    (w1_codes[b][:, cols].bitcast(FP8X4), w1_sc[b], a2_ring),
+                    (w4[b][:, 2 * P * i : 2 * P * (i + 1)].bitcast(FP4X4), w4_sc[b], b2_ring),
+                ):
+                    acc = next_bank()
+                    nc.tensor.matmul_mx(
+                        out=acc[:], lhsT=codes, lhsT_scale=scales[:, cols],
+                        rhs=v_codes[half][:].bitcast(FP8X4), rhs_scale=v_sc[half][:], start=True, stop=True,
+                    )
+                    nc.scalar.activation(out=squared[s % AHEAD][:, chunk(half)], in_=acc[:], func=ACT.Square)
 
-        neg_h = {}
-        gap = held("gap", S, F32)
+        def difference(s, engine, halves):
+            j = s % AHEAD
+            for half in halves:
+                cols = chunk(half)
+                engine.tensor_tensor(out=neg_h[:, cols], in0=b2_ring[j][:, cols], in1=a2_ring[j][:, cols], op=ALU.subtract)
+            for half in halves:
+                cols = chunk(half)
+                engine.tensor_tensor(out=weighted[j][:, cols], in0=neg_h[:, cols], in1=wgt[:, cols], op=ALU.mult)
 
-        def difference(s, lo, hi, eng=nc.gpsimd):
-            a2, b2 = sq[s]
-            neg_h[s] = h_ring[s % 3]
-            eng.tensor_tensor(out=gap[:, lo:hi], in0=b2[:, lo:hi], in1=a2[:, lo:hi], op=ALU.subtract)
-            eng.tensor_tensor(out=neg_h[s][:, lo:hi], in0=gap[:, lo:hi], in1=wgt[:, lo:hi], op=ALU.mult)
+        def scatter(s):
+            nc.vector.tensor_copy(out=pages[s % PAGES][:].indirect(places[:]), in_=weighted[s % AHEAD][:])
 
-        def scatter(s, lo, hi):
-            window = pages[s % 4][:].indirect(places[:, lo // 16 : hi // 16])
-            nc.vector.tensor_copy(out=window, in_=neg_h[s][:, lo:hi])
-
-        z_turned = [[held("z_turned%d_%d" % (u, k), 512, BF16) for k in range(8)] for u in range(2)]
-        z_words = {(0, c): held("z_words0_%d" % c, 2048, BF16) for c in range(4)}
-        z_codes = {(1, c): held("z_codes1_%d" % c, BANK, U32)[:] for c in range(4)}
-        z_sc = [[held("z_sc%d_%d" % (b, c), BANK, U8) for c in range(4)] for b in range(2)]
+        z_turned = [[held("z_turned%d_%d" % (u, k), BANK, BF16) for k in range(STRIPS)] for u in range(2)]
+        z_in = {(0, c): held("z_in0_%d" % c, PACK * BANK, BF16) for c in range(CHUNKS)}
+        z_codes = {(1, c): held("z_codes1_%d" % c, BANK, U32)[:] for c in range(CHUNKS)}
+        z_sc = {
+            (b, c): held("z_sc%d_%d" % (b, c), BANK, U8)[:]
+            for c in range(CHUNKS)
+            for b in range(2)
+            if b == 1 or c >= FIRST_CHUNKS
+        }
         pairs = {}
 
         def turn(b, u, k):
-            acc = next_bank()[:].rearrange("q (mm e p) -> q mm e p", mm=2, e=2)
-            for mm in range(2):
-                cols = slice(P * (2 * k + mm), P * (2 * k + mm + 1))
+            acc = next_bank()[:].rearrange("m (blk e p) -> m blk e p", blk=2, e=2)
+            for blk in range(2):
+                cols = slice(P * (2 * k + blk), P * (2 * k + blk + 1))
                 for e in range(2):
-                    s = 4 * b + 2 * u + e
-                    nc.tensor.matmul(acc[:, mm, e, :], lhsT=pages[s % 4][:, cols], rhs=ident[:], is_transpose=True, start=True, stop=False)
-                    nc.tensor.matmul(acc[:, mm, e, :], lhsT=rec[s][:, cols], rhs=ident[:], is_transpose=True, start=False, stop=True)
-            dst = z_turned[u][k][:].rearrange("q (mm p e) -> q mm p e", mm=2, e=2)
-            nc.scalar.copy(out=dst, in_=acc.rearrange("q mm e p -> q mm p e"))
+                    j = (PACK * b + 2 * u + e) % PAGES
+                    for term, first in ((pages[j], True), (rec[j], False)):
+                        nc.tensor.matmul(
+                            acc[:, blk, e, :], lhsT=term[:, cols], rhs=ident[:],
+                            is_transpose=True, start=first, stop=not first,
+                        )
+            nc.scalar.copy(
+                out=z_turned[u][k][:].rearrange("m (blk p e) -> m blk p e", blk=2, e=2),
+                in_=acc.rearrange("m blk e p -> m blk p e"),
+            )
 
         def turn_back(k):
-            acc = next_bank()[:].rearrange("p (u mm m) -> p u mm m", u=2, mm=2)
+            acc = next_bank()[:].rearrange("p (u blk m) -> p u blk m", u=2, blk=2)
             for u in range(2):
                 words = z_turned[u][k][:].bitcast(F32)
-                for mm in range(2):
-                    nc.tensor.transpose(acc[:, u, mm, :], words[:, P * mm : P * (mm + 1)], ident[:])
-            dst = z_words[0, k // 2][:].bitcast(F32)[:, BANK * (k % 2) : BANK * (k % 2 + 1)]
-            nc.scalar.copy(out=dst.rearrange("p (m u) -> p m u", u=2), in_=acc.rearrange("p u mm m -> p (mm m) u"))
+                for blk in range(2):
+                    nc.tensor.transpose(acc[:, u, blk, :], words[:, P * blk : P * (blk + 1)], ident[:])
+            nc.scalar.copy(
+                out=z_in[0, k // 2][:].bitcast(F32)[:, chunk(k % 2)].rearrange("p (m u) -> p m u", u=2),
+                in_=acc.rearrange("p u blk m -> p (blk m) u"),
+            )
 
         def turn_back_pair(c):
             acc = next_bank()
-            for mb in range(4):
-                words = z_turned[0][2 * c + mb // 2][:].bitcast(F32)
-                nc.tensor.transpose(acc[:, P * mb : P * (mb + 1)], words[:, P * (mb % 2) : P * (mb % 2 + 1)], ident[:])
-            nc.scalar.copy(out=pairs[c][:].bitcast(F32)[:, 0:BANK], in_=acc[:])
+            for blk in range(4):
+                words = z_turned[0][2 * c + blk // 2][:].bitcast(F32)
+                nc.tensor.transpose(acc[:, P * blk : P * (blk + 1)], words[:, P * (blk % 2) : P * (blk % 2 + 1)], ident[:])
+            nc.scalar.copy(out=pairs[c][:].bitcast(F32)[:, chunk(0)], in_=acc[:])
 
-        def quantize_z(b, c):
-            nc.vector.quantize_mx(out=z_codes[b, c].bitcast(FP8X4), scales=z_sc[b][c][:], in_=z_words[b, c][:])
-
-        def chunk(c):
-            return slice(BANK * c, BANK * (c + 1))
-
-        planes = {}
-
-        def pair_tag(c):
-            return ("w1_then_pairs%d" if c < PE_CHUNKS else "z_turned0_%d") % c
-
-        def plane_sum(s, c):
-            at = c if s == 6 else 2 * (c - PE_CHUNKS) + s % 2
-            nc.gpsimd.tensor_tensor(
-                out=planes[s // 2][:, chunk(at)], in0=rec[s][:, chunk(c)], in1=pages[s % 4][:, chunk(c)], op=ALU.add
-            )
-
-        def pair_slots(u, c):
+        def pair_values(u, c):
             return pairs[c][:, 2 * BANK * u : 2 * BANK * (u + 1)].rearrange("p (m e) -> p m e", e=2)
 
-        def last_sum(c):
-            nc.vector.tensor_tensor(out=pair_slots(1, c)[:, :, 1], in0=rec[7][:, chunk(c)], in1=pages[3][:, chunk(c)], op=ALU.add)
+        def sum_on_gpsimd(dst, s, c):
+            j = s % PAGES
+            nc.gpsimd.tensor_tensor(out=dst, in0=rec[j][:, chunk(c)], in1=pages[j][:, chunk(c)], op=ALU.add)
 
-        def last_weave(c):
-            z_words[1, c] = held("z_words1_%d" % c, 2048, BF16)
+        def last_sum(c):
+            j = (SLICES - 1) % PAGES
+            nc.vector.tensor_tensor(
+                out=pair_values(1, c)[:, :, 1], in0=rec[j][:, chunk(c)], in1=pages[j][:, chunk(c)], op=ALU.add
+            )
+
+        def interleave_pairs(c):
+            z_in[1, c] = held("z_in1_%d" % c, PACK * BANK, BF16)
             nc.vector.tensor_copy(
-                out=z_words[1, c][:].bitcast(F32).rearrange("p (m u) -> p m u", u=2),
+                out=z_in[1, c][:].bitcast(F32).rearrange("p (m u) -> p m u", u=2),
                 in_=pairs[c][:].bitcast(F32).rearrange("p (u m) -> p m u", u=2),
             )
 
-        squashed = {}
+        def quantize_z(b, c):
+            nc.vector.quantize_mx(out=z_codes[b, c].bitcast(FP8X4), scales=z_sc[b, c], in_=z_in[b, c][:])
+
+        results = {}
 
         def commands(c):
-            result = held("result%d" % c, T2, F32, ("w4_sc_raw", "tab_sc", "page0", "page1")[c])
-            for nt in range(4):
+            staged = held("staged%d" % c, T2, F32, ("w1_bf0", "w1_bf1", "page0", "page1")[c])
+            for nt in range(N // P):
                 acc = banks[(4 + 4 * c + nt) % 8]
                 for b in range(2):
                     cols = slice(N * b + P * nt, N * b + P * (nt + 1))
                     nc.tensor.matmul_mx(
                         out=acc[:], lhsT=w8[:, cols].bitcast(FP8X4), lhsT_scale=w8_sc[:, cols],
-                        rhs=z_codes[b, c].bitcast(FP8X4), rhs_scale=z_sc[b][c][:], start=(b == 0), stop=(b == 1),
+                        rhs=z_codes[b, c].bitcast(FP8X4), rhs_scale=z_sc[b, c], start=(b == 0), stop=(b == 1),
                     )
-                squashed[c, nt] = result[:, chunk(nt)]
-                nc.scalar.activation(out=squashed[c, nt], in_=acc[:], func=ACT.Tanh)
+                results[c, nt] = staged[:, chunk(nt)]
+                nc.scalar.activation(out=results[c, nt], in_=acc[:], func=ACT.Tanh)
 
-        def limit(c, nt, on_scalar):
-            res = squashed[c, nt]
-            if on_scalar:
-                nc.scalar.activation(out=res, in_=res, func=ACT.Copy, scale=lim_col[:, nt : nt + 1])
-            else:
-                nc.vector.tensor_scalar(
-                    out=res, in0=res, scalar1=lim_col[:, nt : nt + 1], scalar2=None, op0=ALU.mult
-                )
-            nc.sync.dma_start(out=out[P * nt : P * (nt + 1), chunk(c)], in_=res)
+        def limit(c, on_scalar):
+            for nt in range(N // P):
+                if ((c, nt) in SCALAR_LIMITS) == on_scalar:
+                    res, factor = results[c, nt], lim_col[:, nt : nt + 1]
+                    if on_scalar:
+                        nc.scalar.activation(out=res, in_=res, func=ACT.Copy, scale=factor)
+                    else:
+                        nc.vector.tensor_scalar(out=res, in0=res, scalar1=factor, scalar2=None, op0=ALU.mult)
+                    nc.sync.dma_start(out=out[P * nt : P * (nt + 1), chunk(c)], in_=res)
 
         round_w1(0)
         order_w4_words(0)
         order_w4_words(1)
         wgt = held("wgt", S, F32, "w4_raw")
         nc.sync.dma_start(out=wgt[:], in_=wgs)
+        gather_words(0)
+        gather_words(1)
         gather_scales(0)
         gather_scales(1)
         quantize_w1(0)
-        gather_words(0)
         order_w4_scales(0)
         order_w4_scales(1)
-        gather_words(1)
-        load_w1(2)
-        load_w1(3)
-        rec_ring.append(held("rec0", T2, F32, "w4_sc_raw"))
-        rec_ring.append(held("rec1", T2, F32, "tab_sc"))
+        load_w1(1)
+        rec.append(held("rec0", T2, F32, "w1_bf0"))
         load_recipe(0)
-        load_recipe(1)
-        pages.append(held("page2", T2, F32, "tab_then_page"))
-        pages.append(held("page3", T2, F32, "w1_then_page"))
+        pages.append(held("page2", T2, F32, "tab"))
+        pages.append(held("page3", T2, F32, "w4_sc_raw"))
         for page in pages[2:]:
             nc.gpsimd.memset(page[:], 0.0)
         squares(0)
-        difference(0, 0, BANK, nc.vector)
+        difference(0, nc.vector, [0])
+        difference(0, nc.vector, [1])
         squares(1)
-        difference(0, BANK, S)
-        scatter(0, 0, BANK)
+        w1_bf.append(held("w1_bf1", PACK * BANK, BF16))
         round_w1(1)
-        for c in range(PE_CHUNKS):
-            pairs[c] = held("pairs%d" % c, 2048, BF16, "w1_then_pairs%d" % c)
         squares(2)
         squares(3)
-        difference(1, 0, S)
-        difference(2, 0, S)
-        scatter(0, BANK, S)
+        difference(1, nc.gpsimd, [0, 1])
+        difference(2, nc.gpsimd, [0, 1])
+        scatter(0)
         quantize_w1(1)
-        rec_ring.append(held("rec2", T2, F32, "w1_bf1"))
-        rec_ring.append(held("rec3", T2, F32, "w4_0"))
-        load_recipe(2)
-        load_recipe(3)
-        w8 = held("w8", 2 * N, I32, "w1_codes0")
-        w8_sc = held("w8_sc", 2 * N, U8, "w1_sc0")
-        lim_col = held("lim_col", N // P, F32, "w4_sc0")
+        rec.append(held("rec1", T2, F32, "w1_bf1"))
+        rec.append(held("rec2", T2, F32, "w4_0"))
+        rec.append(held("rec3", T2, F32, "w1_codes0"))
+        for s in range(1, PAGES):
+            load_recipe(s)
+        squares(4)
+        squares(5)
+
+        def step(s):
+            if s + 2 < SLICES:
+                difference(s + 2, nc.gpsimd, [0, 1])
+            scatter(s)
+
+        step(1)
+        for k in range(STRIPS):
+            turn(0, 0, k)
+        load_recipe(4)
+        load_recipe(5)
+        step(2)
+        squares(6)
+        squares(7)
+        w8 = held("w8", 2 * N, I32, "w1_codes1")
+        w8_sc = held("w8_sc", 2 * N, U8, "w1_sc1")
+        lim_col = held("lim_col", N // P, F32, "w4_sc1")
         nc.gpsimd.memset(w8_sc[:].bitcast(I32), 0)
         nc.sync.dma_start(
             out=w8[:].rearrange("p (a c) -> p a c", a=2),
@@ -293,59 +321,58 @@ def tile_list_wafer_overlay_correction_kernel(
         )
         for q in range(4):
             nc.sync.dma_start(
-                out=w8_sc[32 * q : 32 * q + 4, :].bitcast(I32).rearrange("p (a c) -> p a c", a=2),
+                out=scale_rows(w8_sc, q).rearrange("p (a c) -> p a c", a=2),
                 in_=w8_scales[:, 4 * q : 4 * q + 4, :].rearrange("a r c -> r a c").bitcast(I32),
             )
         with nc.allow_non_contiguous_dma(reason="one limit for each partition"):
-            nc.sync.dma_start(out=lim_col[:], in_=lim.rearrange("(c p) -> p c", p=P))
-        squares(4)
-        squares(5)
-        for s in range(1, SLICES):
-            if s + 2 < SLICES:
-                difference(s + 2, 0, S)
-            scatter(s, 0, S)
-            if s in (1, 3):
-                for k in range(8):
-                    turn(0, s // 2, k)
-                load_recipe(s + 3)
-                load_recipe(s + 4)
-            if s == 2:
-                squares(6)
-                squares(7)
-            if s == 3:
-                for k in range(8):
-                    turn_back(k)
-            if s == 5:
-                for k in range(2 * PE_CHUNKS):
-                    turn(1, 0, k)
-                for c in range(PE_CHUNKS):
-                    turn_back_pair(c)
-            if s == 6:
-                planes[2] = held("planes45", T2, BF16, "gap")
-                planes[3] = held("plane6", T2, BF16, "z_turned0_1")
-                for c in range(PE_CHUNKS, 4):
-                    pairs[c] = held("pairs%d" % c, 2048, BF16, "z_turned0_%d" % c)
-                for c in range(PE_CHUNKS, 4):
-                    plane_sum(4, c)
-                for c in range(PE_CHUNKS, 4):
-                    plane_sum(5, c)
-                    nc.scalar.copy(out=pair_slots(0, c), in_=planes[2][:, 2 * BANK * (c - PE_CHUNKS) : 2 * BANK * (c - PE_CHUNKS + 1)].rearrange("p (e m) -> p m e", e=2))
-                for c in range(4):
-                    plane_sum(6, c)
-                    nc.scalar.copy(out=pair_slots(1, c), in_=planes[3][:, chunk(c)].unsqueeze(2).to_broadcast([P, BANK, 2]))
-        last_sum(0)
-        for c in range(4):
-            last_weave(c)
-            z_codes[0, c] = held("z_codes0_%d" % c, BANK, U32, pair_tag(c))[:]
+            nc.sync.dma_start(out=lim_col[:], in_=lim.rearrange("(nt p) -> p nt", p=P))
+        step(3)
+        for k in range(STRIPS):
+            turn(0, 1, k)
+        load_recipe(6)
+        load_recipe(7)
+        for k in range(STRIPS):
+            turn_back(k)
+        step(4)
+        step(5)
+        pair_bytes = ("w1_raw0", "z_turned0_0", "z_turned0_7", "z_turned1_7")
+        for c in range(TURNED_CHUNKS):
+            pairs[c] = held("pairs%d" % c, PACK * BANK, BF16, pair_bytes[c])
+            turn(1, 0, 2 * c)
+            turn(1, 0, 2 * c + 1)
+            turn_back_pair(c)
+        step(6)
+        z45_tile = held("z45", 2 * BANK * (CHUNKS - TURNED_CHUNKS), BF16, "neg_h")
+        z45 = z45_tile[:].rearrange("p (c e m) -> p c e m", e=2, m=BANK)
+        z6 = held("z6", T2, BF16)
+        for c in range(TURNED_CHUNKS, CHUNKS):
+            pairs[c] = held("pairs%d" % c, PACK * BANK, BF16, pair_bytes[c])
+            sum_on_gpsimd(z45[:, c - TURNED_CHUNKS, 0, :], 4, c)
+        for c in range(TURNED_CHUNKS, CHUNKS):
+            sum_on_gpsimd(z45[:, c - TURNED_CHUNKS, 1, :], 5, c)
+            nc.scalar.copy(out=pair_values(0, c), in_=z45[:, c - TURNED_CHUNKS].rearrange("p e m -> p m e"))
+        for c in range(CHUNKS):
+            sum_on_gpsimd(z6[:, chunk(c)], 6, c)
+            nc.scalar.copy(out=pair_values(1, c), in_=z6[:, chunk(c)].unsqueeze(2).to_broadcast([P, BANK, 2]))
+        step(7)
+
+        first_codes = held("first_codes", FIRST_CHUNKS * BANK, U32, "weighted%d" % ((SLICES - 1) % AHEAD))
+        first_sc = held("first_sc", FIRST_CHUNKS * BANK, U8, "z_turned0_1")
+        for c in range(FIRST_CHUNKS):
+            z_sc[0, c] = first_sc[:, chunk(c)]
+            z_codes[0, c] = first_codes[:, chunk(c)]
             quantize_z(0, c)
+        last_sum(0)
+        for c in range(CHUNKS):
+            interleave_pairs(c)
+            if c >= FIRST_CHUNKS:
+                z_codes[0, c] = held("z_codes0_%d" % c, BANK, U32, pair_bytes[c])[:]
+                quantize_z(0, c)
             quantize_z(1, c)
-            if c + 1 < 4:
+            if c + 1 < CHUNKS:
                 last_sum(c + 1)
             commands(c)
             if c >= 1:
-                for nt in range(3):
-                    limit(c - 1, nt, False)
-            if c + 1 < 4:
-                limit(c, 3, True)
-        for nt in range(4):
-            limit(3, nt, False)
+                limit(c - 1, on_scalar=False)
+            limit(c, on_scalar=True)
+        limit(CHUNKS - 1, on_scalar=False)

from contextlib import ExitStack

import concourse.mybir as mybir
from concourse.masks import make_identity

T, S, T2, K, H, N = 2048, 1024, 2048, 512, 1024, 512
FLOPS = 2 * (2 * K * H * S + H * N * T2)

F32 = mybir.dt.float32
BF16 = mybir.dt.bfloat16
I32 = mybir.dt.int32
U32 = mybir.dt.uint32
U16 = mybir.dt.uint16
U8 = mybir.dt.uint8
FP8X4 = mybir.dt.float8_e4m3fn_x4
FP4X4 = mybir.dt.float4_e2m1fn_x4
ACT = mybir.ActivationFunctionType
ALU = mybir.AluOpType

P = 128
BANK = 512
PACK = 4
SLICES = H // P
CHUNKS = T2 // BANK
STRIPS = T2 // (2 * P)
W1_COLS = 256
PAGES = 4
AHEAD = 3
TURNED_CHUNKS = 1
SCALAR_LIMITS = [(c, nt) for c in range(2) for nt in (2, 3)]
FIRST_CHUNKS = 2


def tile_list_wafer_overlay_correction_kernel(
    tc, tab_words, tab_scales, offs, offs2, w1, w4_words, w4_scales, wgs, recipe, w8_words, w8_scales, lim, out
):
    nc = tc.nc
    with ExitStack() as ctx:
        lists = ctx.enter_context(tc.tile_pool(name="lists", bufs=1))
        keep = ctx.enter_context(tc.tile_pool(name="keep", bufs=1))
        psum = ctx.enter_context(tc.psum_pool(name="psum", bufs=1))
        banks = [psum.tile([P, BANK], F32, name="bank%d" % j) for j in range(8)]
        taken = []

        def next_bank():
            taken.append(len(taken))
            return banks[taken[-1] % 4]

        def held(name, cols, dtype, after=None):
            return keep.tile([P, cols], dtype, name=name, tag=after or name, align_bytes=64)

        def chunk(c):
            return slice(BANK * c, BANK * (c + 1))

        def scale_rows(plane, q):
            return plane[32 * q : 32 * q + 4, :].bitcast(I32)

        picks = lists.tile([P, S // 16], U16, name="picks")
        places = lists.tile([P, S // 16], U16, name="places")
        tab = held("tab", T, I32)
        tab_sc = held("tab_sc", T, U8)
        w4_raw = held("w4_raw", 2 * H, U8)
        w4_sc_raw = held("w4_sc_raw", H, U8)
        ident = held("ident", P, F32)
        w1_raw = [keep.tile([P, PACK, W1_COLS], F32, name="w1_raw%d" % j, align_bytes=64) for j in range(2)]

        nc.vector.memset(tab_sc[:].bitcast(I32), 0)
        pages = [held("page0", T2, F32), held("page1", T2, F32)]
        for page in pages:
            nc.vector.memset(page[:], 0.0)
        nc.vector.memset(w4_sc_raw[:].bitcast(I32), 0)
        make_identity(nc, ident[:])

        def load_w1(b):
            for j in range(2):
                cols = slice(BANK * b + W1_COLS * j, BANK * b + W1_COLS * (j + 1))
                nc.sync.dma_start(out=w1_raw[j][:], in_=w1[:, cols].rearrange("(p t) c -> p t c", t=PACK))

        nc.sync.dma_start(picks[:], offs)
        nc.sync.dma_start(out=w4_raw[:].bitcast(I32), in_=w4_words[0].bitcast(I32))
        nc.sync.dma_start(out=tab[:], in_=tab_words[0].rearrange("p t i -> p (t i)").bitcast(I32))
        nc.sync.dma_start(places[:], offs2)
        load_w1(0)
        for q in range(4):
            nc.scalar.dma_start(out=scale_rows(tab_sc, q), in_=tab_scales[0, 4 * q : 4 * q + 4, :].bitcast(I32))
        for q in range(4):
            nc.sync.dma_start(out=scale_rows(w4_sc_raw, q), in_=w4_scales[0, 4 * q : 4 * q + 4, :].bitcast(I32))

        recipe_slices = recipe.rearrange("(b p i) m -> b i p m", b=2, i=PACK)
        rec = []

        def load_recipe(s):
            nc.sync.dma_start(out=rec[s % PAGES][:], in_=recipe_slices[s // PACK, s % PACK])

        v_codes = [held("v_codes%d" % half, BANK, U32) for half in range(2)]
        v_sc = [held("v_sc%d" % half, BANK, U8) for half in range(2)]

        def entries(half):
            return picks[:, BANK // 16 * half : BANK // 16 * (half + 1)]

        def gather_words(half):
            nc.vector.tensor_copy(out=v_codes[half][:], in_=tab[:].bitcast(U32).indirect(entries(half)))

        def gather_scales(half):
            nc.vector.tensor_copy(out=v_sc[half][:], in_=tab_sc[:].indirect(entries(half)))

        w1_bf = [held("w1_bf0", PACK * BANK, BF16)]
        w1_codes = [held("w1_codes%d" % b, BANK, U32) for b in range(2)]
        w1_sc = [held("w1_sc%d" % b, BANK, U8) for b in range(2)]
        w4 = [held("w4_%d" % b, 2 * BANK, U8) for b in range(2)]
        w4_sc = [held("w4_sc%d" % b, BANK, U8) for b in range(2)]

        def round_w1(b):
            grouped = w1_bf[b][:].rearrange("p (i c t) -> p c i t", i=PACK, t=PACK)
            width = W1_COLS // PACK
            for j in range(2):
                nc.scalar.copy(
                    out=grouped[:, width * j : width * (j + 1)],
                    in_=w1_raw[j][:].rearrange("p t (c i) -> p c i t", i=PACK),
                )

        def quantize_w1(b):
            nc.vector.quantize_mx(out=w1_codes[b][:].bitcast(FP8X4), scales=w1_sc[b][:], in_=w1_bf[b][:])

        def order_w4_words(b):
            nc.vector.tensor_copy(
                out=w4[b][:].bitcast(U16).rearrange("p (i c) -> p i c", i=PACK),
                in_=w4_raw[:].bitcast(U16)[:, chunk(b)].rearrange("p (c i) -> p i c", i=PACK),
            )

        def order_w4_scales(b):
            nc.vector.tensor_copy(
                out=w4_sc[b][:].rearrange("p (i c) -> p i c", i=PACK),
                in_=w4_sc_raw[:, chunk(b)].rearrange("p (c i) -> p i c", i=PACK),
            )

        a2_ring = [held("a2_%d" % j, S, F32) for j in range(AHEAD)]
        b2_ring = [held("b2_%d" % j, S, F32) for j in range(AHEAD)]
        weighted = [held("weighted%d" % j, S, F32) for j in range(AHEAD)]
        neg_h = held("neg_h", S, F32)

        def squares(s):
            b, i = divmod(s, PACK)
            cols = slice(P * i, P * (i + 1))
            for half in range(2):
                for codes, scales, squared in (
                    (w1_codes[b][:, cols].bitcast(FP8X4), w1_sc[b], a2_ring),
                    (w4[b][:, 2 * P * i : 2 * P * (i + 1)].bitcast(FP4X4), w4_sc[b], b2_ring),
                ):
                    acc = next_bank()
                    nc.tensor.matmul_mx(
                        out=acc[:], lhsT=codes, lhsT_scale=scales[:, cols],
                        rhs=v_codes[half][:].bitcast(FP8X4), rhs_scale=v_sc[half][:], start=True, stop=True,
                    )
                    nc.scalar.activation(out=squared[s % AHEAD][:, chunk(half)], in_=acc[:], func=ACT.Square)

        def difference(s, engine, halves):
            j = s % AHEAD
            for half in halves:
                cols = chunk(half)
                engine.tensor_tensor(out=neg_h[:, cols], in0=b2_ring[j][:, cols], in1=a2_ring[j][:, cols], op=ALU.subtract)
            for half in halves:
                cols = chunk(half)
                engine.tensor_tensor(out=weighted[j][:, cols], in0=neg_h[:, cols], in1=wgt[:, cols], op=ALU.mult)

        def scatter(s):
            nc.vector.tensor_copy(out=pages[s % PAGES][:].indirect(places[:]), in_=weighted[s % AHEAD][:])

        z_turned = [[held("z_turned%d_%d" % (u, k), BANK, BF16) for k in range(STRIPS)] for u in range(2)]
        z_in = {(0, c): held("z_in0_%d" % c, PACK * BANK, BF16) for c in range(CHUNKS)}
        z_codes = {(1, c): held("z_codes1_%d" % c, BANK, U32)[:] for c in range(CHUNKS)}
        z_sc = {
            (b, c): held("z_sc%d_%d" % (b, c), BANK, U8)[:]
            for c in range(CHUNKS)
            for b in range(2)
            if b == 1 or c >= FIRST_CHUNKS
        }
        pairs = {}

        def turn(b, u, k):
            acc = next_bank()[:].rearrange("m (blk e p) -> m blk e p", blk=2, e=2)
            for blk in range(2):
                cols = slice(P * (2 * k + blk), P * (2 * k + blk + 1))
                for e in range(2):
                    j = (PACK * b + 2 * u + e) % PAGES
                    for term, first in ((pages[j], True), (rec[j], False)):
                        nc.tensor.matmul(
                            acc[:, blk, e, :], lhsT=term[:, cols], rhs=ident[:],
                            is_transpose=True, start=first, stop=not first,
                        )
            nc.scalar.copy(
                out=z_turned[u][k][:].rearrange("m (blk p e) -> m blk p e", blk=2, e=2),
                in_=acc.rearrange("m blk e p -> m blk p e"),
            )

        def turn_back(k):
            acc = next_bank()[:].rearrange("p (u blk m) -> p u blk m", u=2, blk=2)
            for u in range(2):
                words = z_turned[u][k][:].bitcast(F32)
                for blk in range(2):
                    nc.tensor.transpose(acc[:, u, blk, :], words[:, P * blk : P * (blk + 1)], ident[:])
            nc.scalar.copy(
                out=z_in[0, k // 2][:].bitcast(F32)[:, chunk(k % 2)].rearrange("p (m u) -> p m u", u=2),
                in_=acc.rearrange("p u blk m -> p (blk m) u"),
            )

        def turn_back_pair(c):
            acc = next_bank()
            for blk in range(4):
                words = z_turned[0][2 * c + blk // 2][:].bitcast(F32)
                nc.tensor.transpose(acc[:, P * blk : P * (blk + 1)], words[:, P * (blk % 2) : P * (blk % 2 + 1)], ident[:])
            nc.scalar.copy(out=pairs[c][:].bitcast(F32)[:, chunk(0)], in_=acc[:])

        def pair_values(u, c):
            return pairs[c][:, 2 * BANK * u : 2 * BANK * (u + 1)].rearrange("p (m e) -> p m e", e=2)

        def sum_on_gpsimd(dst, s, c):
            j = s % PAGES
            nc.gpsimd.tensor_tensor(out=dst, in0=rec[j][:, chunk(c)], in1=pages[j][:, chunk(c)], op=ALU.add)

        def last_sum(c):
            j = (SLICES - 1) % PAGES
            nc.vector.tensor_tensor(
                out=pair_values(1, c)[:, :, 1], in0=rec[j][:, chunk(c)], in1=pages[j][:, chunk(c)], op=ALU.add
            )

        def interleave_pairs(c):
            z_in[1, c] = held("z_in1_%d" % c, PACK * BANK, BF16)
            nc.vector.tensor_copy(
                out=z_in[1, c][:].bitcast(F32).rearrange("p (m u) -> p m u", u=2),
                in_=pairs[c][:].bitcast(F32).rearrange("p (u m) -> p m u", u=2),
            )

        def quantize_z(b, c):
            nc.vector.quantize_mx(out=z_codes[b, c].bitcast(FP8X4), scales=z_sc[b, c], in_=z_in[b, c][:])

        results = {}

        def commands(c):
            staged = held("staged%d" % c, T2, F32, ("w1_bf0", "w1_bf1", "page0", "page1")[c])
            for nt in range(N // P):
                acc = banks[(4 + 4 * c + nt) % 8]
                for b in range(2):
                    cols = slice(N * b + P * nt, N * b + P * (nt + 1))
                    nc.tensor.matmul_mx(
                        out=acc[:], lhsT=w8[:, cols].bitcast(FP8X4), lhsT_scale=w8_sc[:, cols],
                        rhs=z_codes[b, c].bitcast(FP8X4), rhs_scale=z_sc[b, c], start=(b == 0), stop=(b == 1),
                    )
                results[c, nt] = staged[:, chunk(nt)]
                nc.scalar.activation(out=results[c, nt], in_=acc[:], func=ACT.Tanh)

        def limit(c, on_scalar):
            for nt in range(N // P):
                if ((c, nt) in SCALAR_LIMITS) == on_scalar:
                    res, factor = results[c, nt], lim_col[:, nt : nt + 1]
                    if on_scalar:
                        nc.scalar.activation(out=res, in_=res, func=ACT.Copy, scale=factor)
                    else:
                        nc.vector.tensor_scalar(out=res, in0=res, scalar1=factor, scalar2=None, op0=ALU.mult)
                    nc.sync.dma_start(out=out[P * nt : P * (nt + 1), chunk(c)], in_=res)

        round_w1(0)
        order_w4_words(0)
        order_w4_words(1)
        wgt = held("wgt", S, F32, "w4_raw")
        nc.sync.dma_start(out=wgt[:], in_=wgs)
        gather_words(0)
        gather_words(1)
        gather_scales(0)
        gather_scales(1)
        quantize_w1(0)
        order_w4_scales(0)
        order_w4_scales(1)
        load_w1(1)
        rec.append(held("rec0", T2, F32, "w1_bf0"))
        load_recipe(0)
        pages.append(held("page2", T2, F32, "tab"))
        pages.append(held("page3", T2, F32, "w4_sc_raw"))
        for page in pages[2:]:
            nc.gpsimd.memset(page[:], 0.0)
        squares(0)
        difference(0, nc.vector, [0])
        difference(0, nc.vector, [1])
        squares(1)
        w1_bf.append(held("w1_bf1", PACK * BANK, BF16))
        round_w1(1)
        squares(2)
        squares(3)
        difference(1, nc.gpsimd, [0, 1])
        difference(2, nc.gpsimd, [0, 1])
        scatter(0)
        quantize_w1(1)
        rec.append(held("rec1", T2, F32, "w1_bf1"))
        rec.append(held("rec2", T2, F32, "w4_0"))
        rec.append(held("rec3", T2, F32, "w1_codes0"))
        for s in range(1, PAGES):
            load_recipe(s)
        squares(4)
        squares(5)

        def step(s):
            if s + 2 < SLICES:
                difference(s + 2, nc.gpsimd, [0, 1])
            scatter(s)

        step(1)
        for k in range(STRIPS):
            turn(0, 0, k)
        load_recipe(4)
        load_recipe(5)
        step(2)
        squares(6)
        squares(7)
        w8 = held("w8", 2 * N, I32, "w1_codes1")
        w8_sc = held("w8_sc", 2 * N, U8, "w1_sc1")
        lim_col = held("lim_col", N // P, F32, "w4_sc1")
        nc.gpsimd.memset(w8_sc[:].bitcast(I32), 0)
        nc.sync.dma_start(
            out=w8[:].rearrange("p (a c) -> p a c", a=2),
            in_=w8_words.rearrange("a p c i -> p a (c i)").bitcast(I32),
        )
        for q in range(4):
            nc.sync.dma_start(
                out=scale_rows(w8_sc, q).rearrange("p (a c) -> p a c", a=2),
                in_=w8_scales[:, 4 * q : 4 * q + 4, :].rearrange("a r c -> r a c").bitcast(I32),
            )
        with nc.allow_non_contiguous_dma(reason="one limit for each partition"):
            nc.sync.dma_start(out=lim_col[:], in_=lim.rearrange("(nt p) -> p nt", p=P))
        step(3)
        for k in range(STRIPS):
            turn(0, 1, k)
        load_recipe(6)
        load_recipe(7)
        for k in range(STRIPS):
            turn_back(k)
        step(4)
        step(5)
        pair_bytes = ("w1_raw0", "z_turned0_0", "z_turned0_7", "z_turned1_7")
        for c in range(TURNED_CHUNKS):
            pairs[c] = held("pairs%d" % c, PACK * BANK, BF16, pair_bytes[c])
            turn(1, 0, 2 * c)
            turn(1, 0, 2 * c + 1)
            turn_back_pair(c)
        step(6)
        z45_tile = held("z45", 2 * BANK * (CHUNKS - TURNED_CHUNKS), BF16, "neg_h")
        z45 = z45_tile[:].rearrange("p (c e m) -> p c e m", e=2, m=BANK)
        z6 = held("z6", T2, BF16)
        for c in range(TURNED_CHUNKS, CHUNKS):
            pairs[c] = held("pairs%d" % c, PACK * BANK, BF16, pair_bytes[c])
            sum_on_gpsimd(z45[:, c - TURNED_CHUNKS, 0, :], 4, c)
        for c in range(TURNED_CHUNKS, CHUNKS):
            sum_on_gpsimd(z45[:, c - TURNED_CHUNKS, 1, :], 5, c)
            nc.scalar.copy(out=pair_values(0, c), in_=z45[:, c - TURNED_CHUNKS].rearrange("p e m -> p m e"))
        for c in range(CHUNKS):
            sum_on_gpsimd(z6[:, chunk(c)], 6, c)
            nc.scalar.copy(out=pair_values(1, c), in_=z6[:, chunk(c)].unsqueeze(2).to_broadcast([P, BANK, 2]))
        step(7)

        first_codes = held("first_codes", FIRST_CHUNKS * BANK, U32, "weighted%d" % ((SLICES - 1) % AHEAD))
        first_sc = held("first_sc", FIRST_CHUNKS * BANK, U8, "z_turned0_1")
        for c in range(FIRST_CHUNKS):
            z_sc[0, c] = first_sc[:, chunk(c)]
            z_codes[0, c] = first_codes[:, chunk(c)]
            quantize_z(0, c)
        last_sum(0)
        for c in range(CHUNKS):
            interleave_pairs(c)
            if c >= FIRST_CHUNKS:
                z_codes[0, c] = held("z_codes0_%d" % c, BANK, U32, pair_bytes[c])[:]
                quantize_z(0, c)
            quantize_z(1, c)
            if c + 1 < CHUNKS:
                last_sum(c + 1)
            commands(c)
            if c >= 1:
                limit(c - 1, on_scalar=False)
            limit(c, on_scalar=True)
        limit(CHUNKS - 1, on_scalar=False)
